import numpy as np
import ml_dtypes


def mxq(x, axis, fmt="e4m3"):
    dtype, down = {"e4m3": (ml_dtypes.float8_e4m3fn, 7), "e5m2": (ml_dtypes.float8_e5m2, 14)}[fmt]
    v = np.moveaxis(np.asarray(x, np.float32).astype(ml_dtypes.bfloat16).astype(np.float64), axis, -1)
    blocks = v.reshape(v.shape[:-1] + (-1, 32))
    amax = np.abs(blocks).max(-1, keepdims=True)
    byte = np.maximum(np.where(amax > 0, np.frexp(amax)[1] - 1 + 127, 0) - down, 1)
    scale = np.exp2(byte - 127.0)
    codes = (blocks / scale).astype(np.float32).astype(dtype).astype(np.float64)
    return np.moveaxis((codes * scale).reshape(v.shape), -1, axis)


WIDE = False


def mx_kscale(k):
    if not WIDE:
        return np.ones(k)
    levels = np.array([30, -30])
    if k % 512:
        return np.exp2(np.random.permutation(np.resize(levels, k // 32))).repeat(32)
    a = np.empty((k // 512, 16))
    for p in range(k // 512):
        a[p, :8] = np.random.permutation(np.resize(levels, 8))
        for g in range(8):
            far = levels[np.abs(levels - a[p, g]) >= 10]
            a[p, g + 8] = far[np.random.randint(len(far))]
    return np.exp2(a.ravel()).repeat(32)


def f64(x):
    return np.asarray(x).astype(np.float64)


def striped(idx):
    return np.tile(np.asarray(idx).reshape(-1, 16).T, (8, 1)).astype(np.uint16)


def unstriped(offs):
    return offs[:16].T.reshape(-1).astype(np.int64)


E2M1 = np.array([0.0, 0.5, 1.0, 1.5, 2.0, 3.0, 4.0, 6.0, -0.0, -0.5, -1.0, -1.5, -2.0, -3.0, -4.0, -6.0])


def pack_weight(w, fmt):
    k, n = w.shape
    w = f64(np.asarray(w, np.float32).astype(ml_dtypes.bfloat16)).reshape(k // 32, 32, n)
    amax = np.abs(w).max(1)
    if fmt in ("e4m3", "e5m2"):
        byte = np.frexp(amax)[1] - 1 + 127 - (7 if fmt == "e4m3" else 14)
    else:
        mant, ex = np.frexp(amax / 6.0)
        byte = np.where(mant > 0.5, ex, ex - 1) + 127
    byte = np.clip(np.where(amax > 0, byte, 1), 1, 254)
    scaled = (w * np.exp2(127.0 - byte)[:, None, :]).reshape(k, n).astype(np.float32)
    by_word = np.ascontiguousarray(scaled.reshape(k // 512, 128, 4, n).transpose(0, 1, 3, 2))
    if fmt in ("e4m3", "e5m2"):
        words = by_word.astype(ml_dtypes.float8_e4m3fn if fmt == "e4m3" else ml_dtypes.float8_e5m2).view(np.uint8)
    else:
        c = by_word.astype(ml_dtypes.float4_e2m1fn).view(np.uint8) & 0xF
        words = (c[..., 0::2] | (c[..., 1::2] << 4)).reshape(k // 512, 128, 2 * n)
    return np.ascontiguousarray(words), np.ascontiguousarray(byte.astype(np.uint8).reshape(k // 512, 16, n))


def unpack_weight(words, scales, fmt):
    g, _, n = scales.shape
    words = np.ascontiguousarray(words).reshape(g, 128, n, -1)
    if fmt in ("e4m3", "e5m2"):
        vals = words.view(ml_dtypes.float8_e4m3fn if fmt == "e4m3" else ml_dtypes.float8_e5m2).astype(np.float64)
    else:
        nib = np.empty((g, 128, n, 4), np.uint8)
        nib[..., 0::2] = words & 0xF
        nib[..., 1::2] = words >> 4
        vals = E2M1[nib]
    vals = vals * np.repeat(np.exp2(scales.astype(np.float64) - 127.0), 8, axis=1)[..., None]
    return vals.transpose(0, 1, 3, 2).reshape(g * 512, n)


def bf(x):
    return np.asarray(x, np.float32).astype(ml_dtypes.bfloat16)


def planes(Y):
    r, m = Y.shape
    b = f64(bf(Y)).reshape(r // 32, 32, m)
    amax = np.abs(b).max(1)
    byte = np.clip(np.where(amax > 0, np.frexp(amax)[1] - 1 + 127 - 7, 1), 1, 254)
    codes = (b * np.exp2(127.0 - byte)[:, None, :]).reshape(r, m).astype(np.float32).astype(ml_dtypes.float8_e4m3fn).view(np.uint8)
    words = codes.reshape(r // 512, 128, 4, m).transpose(0, 1, 3, 2)
    return np.ascontiguousarray(words), np.ascontiguousarray(byte.astype(np.uint8).reshape(r // 512, 16, m))


K, T, J, S, R, N, Z = 512, 512, 256, 512, 512, 512, 512


def setup_inputs():
    n = np.random.standard_normal
    idx = np.random.permutation(T)[:J]
    idx2 = np.random.permutation(S)[:J]
    idx3 = np.random.permutation(Z)[:J]
    fk = mx_kscale(K)
    fr = mx_kscale(R)
    wp = pack_weight(n((K, R)) * 1 / np.sqrt(K) * fk[:, None], "e5m2")
    wbp = pack_weight(n((R, N)) * 1 / np.sqrt(R) / fr[:, None], "e4m3")
    return {
        "xa": (n((K, T))).astype(np.float32),
        "xb": (n((K, S))).astype(np.float32),
        "hb": (np.random.uniform(0.2, 0.9, (K, 1))).astype(np.float32),
        "fk": (np.random.uniform(0.5, 2.0, (K, 1)) / fk[:, None]).astype(np.float32),
        "w_words": wp[0],
        "w_scales": wp[1],
        "us": (np.random.uniform(0.5, 1.5, (1, R)) * fr).astype(np.float32),
        "wb_words": wbp[0],
        "wb_scales": wbp[1],
        "tz": (n((N, Z)) * 0.6).astype(np.float32),
        "rw": (np.random.uniform(0.5, 2.0, (1, J))).astype(np.float32),
        "offs": striped(idx),
        "offs2": striped(idx2),
        "offs3": striped(idx3),
    }


def reference(xa, xb, hb, fk, w_words, w_scales, us, wb_words, wb_scales, tz, rw, offs, offs2, offs3):
    idx = unstriped(offs)
    idx2 = unstriped(offs2)
    idx3 = unstriped(offs3)
    wu = unpack_weight(w_words, w_scales, "e5m2")
    wbu = unpack_weight(wb_words, wb_scales, "e4m3")
    u = (f64(xa)[:, idx] - np.minimum(f64(xb)[:, idx2], f64(hb))) * f64(fk)
    uq = mxq(u, 0, "e5m2")
    a = uq.T @ wu
    m1 = np.pad(a, ((0, 0), (1, 0)))[:, :R]
    hr = (a - 0.7 * m1) * f64(us)
    hid = hr.T
    hidq = mxq(hid, 0, "e5m2")
    p = wbu.T @ hidq
    y = np.maximum(p, f64(tz)[:, idx3]) * f64(rw)
    words, scales = planes(y)
    return y, words, scales

@@ -1,0 +1,241 @@
+from contextlib import ExitStack
+
+import concourse.mybir as mybir
+
+K, T, J, R, N = 512, 512, 256, 512, 512
+FLOPS = 2 * J * K * R + 2 * N * R * J
+
+F32 = mybir.dt.float32
+BF16 = mybir.dt.bfloat16
+I32 = mybir.dt.int32
+U32 = mybir.dt.uint32
+U16 = mybir.dt.uint16
+U8 = mybir.dt.uint8
+E4M3 = mybir.dt.float8_e4m3fn_x4
+E5M2 = mybir.dt.float8_e5m2_x4
+ALU = mybir.AluOpType
+COPY = mybir.ActivationFunctionType.Copy
+
+P = 128
+PACK = 4
+HALF = J // 2
+LIST_COLS = J // 16
+WORD_PAD = 8
+BYTE_PAD = 32
+NEIGHBOUR = -0.7
+
+
+def interleave(engine_copy, dst, src):
+    engine_copy(
+        out=dst.rearrange("p (c i) t -> p c t i", i=4),
+        in_=src.rearrange("p t (c i) -> p c t i", i=4),
+    )
+
+
+def tile_list_rows_boundedgaps_neighbours_floored_pl_kernel(
+    tc, xa, xb, hb, fk, w_words, w_scales, us, wb_words, wb_scales, tz, rw, offs, offs2, offs3, out_0, out_1, out_2
+):
+    nc = tc.nc
+    halves = [slice(h * HALF, (h + 1) * HALF) for h in range(2)]
+    list_halves = [slice(h * LIST_COLS // 2, (h + 1) * LIST_COLS // 2) for h in range(2)]
+
+    with ExitStack() as ctx:
+        keep = ctx.enter_context(tc.tile_pool(name="keep", bufs=1))
+        psum = ctx.enter_context(tc.psum_pool(name="psum", bufs=1))
+
+        list_a = keep.tile([P, LIST_COLS], U16, name="list_a")
+        list_b = keep.tile([P, LIST_COLS], U16, name="list_b")
+        list_z = keep.tile([P, LIST_COLS], U16, name="list_z")
+        xb_rows = [keep.tile([P, 2, T], F32, name=f"xb_rows{i}") for i in range(2)]
+        xa_01 = keep.tile([P, 2, T], F32, name="xa_01")
+        xa_2 = keep.tile([P, T], F32, name="xa_2")
+        xa_3 = keep.tile([P, T], F32, name="xa_3")
+        tz_rows = [keep.tile([P, 2, T], F32, name=f"tz_rows{i}") for i in range(2)]
+        hb_sb = keep.tile([P, PACK], F32, name="hb_sb")
+        fk_sb = keep.tile([P, PACK], F32, name="fk_sb")
+        us_sb = keep.tile([P, PACK], F32, name="us_sb")
+        us_prev = keep.tile([P, PACK], F32, name="us_prev")
+        rw_sb = keep.tile([P, J], F32, name="rw_sb")
+        w_raw = keep.tile([P, WORD_PAD + R], U32, name="w_raw")
+        ws_raw = keep.tile([P, BYTE_PAD + R], U8, name="ws_raw")
+        wb_raw = keep.tile([P, N], U32, name="wb_raw")
+        wbs_raw = keep.tile([P, N], U8, name="wbs_raw")
+        w_dealt = keep.tile([P, PACK + 1, P], U32, name="w_dealt", align_bytes=64)
+        ws_dealt = keep.tile([P, PACK + 1, P], U8, name="ws_dealt", align_bytes=64)
+        wb_dealt = keep.tile([P, PACK, P], U32, name="wb_dealt", align_bytes=64)
+        wbs_dealt = keep.tile([P, PACK, P], U8, name="wbs_dealt", align_bytes=64)
+
+        xa_v = xa.rearrange("(p t) c -> p t c", t=PACK)
+        xb_v = xb.rearrange("(p t) c -> p t c", t=PACK)
+        tz_v = tz.rearrange("(p t) c -> p t c", t=PACK)
+        y_v = out_0.rearrange("(p t) j -> p t j", t=PACK)
+
+        nc.vector.memset(ws_raw[:].bitcast(I32), 0)
+        nc.vector.memset(wbs_raw[:].bitcast(I32), 0)
+        nc.vector.memset(w_raw[:, :WORD_PAD], 0)
+
+        nc.sync.dma_start(list_b[:], offs2)
+        nc.sync.dma_start(xb_rows[0][:], xb_v[:, 0:2, :])
+        nc.gpsimd.dma_start(hb_sb[:], hb.rearrange("(p t) o -> p (t o)", t=PACK))
+        nc.gpsimd.dma_start(fk_sb[:], fk.rearrange("(p t) o -> p (t o)", t=PACK))
+        nc.sync.dma_start(xb_rows[1][:], xb_v[:, 2:4, :])
+        for q in range(4):
+            nc.scalar.dma_start(
+                ws_raw[32 * q : 32 * q + 4, BYTE_PAD:].bitcast(I32), w_scales[0, 4 * q : 4 * q + 4, :].bitcast(I32)
+            )
+        nc.sync.dma_start(list_a[:], offs)
+        nc.sync.dma_start(xa_01[:], xa_v[:, 0:2, :])
+        nc.sync.dma_start(xa_2[:], xa_v[:, 2, :])
+        nc.sync.dma_start(xa_3[:], xa_v[:, 3, :])
+        nc.gpsimd.dma_start(us_sb[:], us.rearrange("o (p t) -> p (o t)", t=PACK))
+        nc.sync.dma_start(
+            w_raw[:, WORD_PAD:].bitcast(I32), w_words[0].rearrange("p c t -> p (c t)").bitcast(I32)
+        )
+        for q in range(4):
+            nc.sync.dma_start(
+                wbs_raw[32 * q : 32 * q + 4, :].bitcast(I32), wb_scales[0, 4 * q : 4 * q + 4, :].bitcast(I32)
+            )
+        nc.sync.dma_start(list_z[:], offs3)
+        for i in range(2):
+            nc.sync.dma_start(tz_rows[i][:], tz_v[:, 2 * i : 2 * i + 2, :])
+        nc.sync.dma_start(wb_raw[:].bitcast(I32), wb_words[0].rearrange("p c t -> p (c t)").bitcast(I32))
+        nc.sync.dma_start(rw_sb[:], rw[0].partition_broadcast(P))
+
+        xb_g = keep.tile([P, PACK, J], F32, name="xb_g")
+        bound = keep.tile([P, PACK, J], F32, name="bound")
+        xa_g = keep.tile([P, PACK, J], F32, name="xa_g")
+        u_rows = keep.tile([P, PACK, J], BF16, name="u_rows")
+        for t in range(PACK):
+            window = xb_rows[t // 2][:, t % 2, :].indirect(list_b[:])
+            if t % 2 == 0:
+                nc.scalar.activation(xb_g[:, t, :], window, COPY)
+            else:
+                nc.vector.tensor_copy(xb_g[:, t, :], window)
+            nc.vector.tensor_scalar(
+                bound[:, t, :], xb_g[:, t, :], hb_sb[:, t : t + 1], fk_sb[:, t : t + 1], ALU.min, ALU.mult
+            )
+
+        nc.vector.tensor_copy(
+            ws_dealt[:, 0:PACK, :].rearrange("p t m -> p m t"),
+            ws_raw[:, BYTE_PAD - 1 : BYTE_PAD - 1 + R].rearrange("p (m t) -> p m t", t=PACK),
+        )
+        nc.vector.tensor_copy(ws_dealt[:, PACK, :], ws_raw[:, BYTE_PAD + PACK - 1 :: PACK])
+        nc.vector.tensor_scalar(us_prev[:], us_sb[:], NEIGHBOUR, None, ALU.mult)
+
+        def combine(t, cols):
+            nc.vector.scalar_tensor_tensor(
+                u_rows[:, t, cols], xa_g[:, t, cols], fk_sb[:, t : t + 1], bound[:, t, cols], ALU.mult, ALU.subtract
+            )
+
+        nc.scalar.activation(xa_g[:, 0, :], xa_01[:, 0, :].indirect(list_a[:]), COPY)
+        nc.vector.tensor_copy(xa_g[:, 1, :], xa_01[:, 1, :].indirect(list_a[:]))
+        combine(0, slice(0, J))
+        combine(1, slice(0, J))
+        nc.scalar.activation(xa_g[:, 2, :], xa_2[:].indirect(list_a[:]), COPY)
+        combine(2, slice(0, J))
+        for h in range(2):
+            nc.scalar.activation(xa_g[:, 3, halves[h]], xa_3[:].indirect(list_a[:, list_halves[h]]), COPY)
+        for h in range(2):
+            combine(3, halves[h])
+
+        nc.scalar.copy(
+            w_dealt[:, 0:PACK, :].rearrange("p t m -> p m t"),
+            w_raw[:, WORD_PAD - 1 : WORD_PAD - 1 + R].rearrange("p (m t) -> p m t", t=PACK),
+        )
+        nc.scalar.copy(w_dealt[:, PACK, :], w_raw[:, WORD_PAD + PACK - 1 :: PACK])
+
+        u_in = [keep.tile([P, HALF, PACK], BF16, name=f"u_in{h}", align_bytes=64) for h in range(2)]
+        u_codes = [keep.tile([P, HALF], U32, name=f"u_codes{h}", align_bytes=64) for h in range(2)]
+        u_scales = [keep.tile([P, HALF], U8, name=f"u_scales{h}", align_bytes=64) for h in range(2)]
+        for h in range(2):
+            interleave(nc.vector.tensor_copy, u_in[h][:], u_rows[:, :, halves[h]])
+        for h in range(2):
+            nc.vector.quantize_mx(
+                out=u_codes[h][:].bitcast(E5M2), scales=u_scales[h][:], in_=u_in[h][:].rearrange("p j t -> p (j t)")
+            )
+
+        a_before = [psum.tile([P, PACK, HALF], F32, name=f"a_before{h}") for h in range(2)]
+        a_last = [psum.tile([P, HALF], F32, name=f"a_last{h}") for h in range(2)]
+        sums = [[a_before[h][:, s, :] for s in range(PACK)] + [a_last[h][:]] for h in range(2)]
+        for h in range(2):
+            for s in range(PACK + 1):
+                nc.tensor.matmul_mx(
+                    out=sums[h][s],
+                    lhsT=w_dealt[:, s, :].bitcast(E5M2),
+                    lhsT_scale=ws_dealt[:, s, :],
+                    rhs=u_codes[h][:].bitcast(E5M2),
+                    rhs_scale=u_scales[h][:],
+                    start=True,
+                    stop=True,
+                )
+
+        tz_g = keep.tile([P, PACK, J], F32, name="tz_g")
+        nc.vector.tensor_copy(
+            wbs_dealt[:].rearrange("p t m -> p m t"), wbs_raw[:].rearrange("p (m t) -> p m t", t=PACK)
+        )
+        nc.vector.tensor_copy(tz_g[:, 0, :], tz_rows[0][:, 0, :].indirect(list_z[:]))
+        nc.scalar.activation(tz_g[:, 1, :], tz_rows[0][:, 1, :].indirect(list_z[:]), COPY)
+
+        taken = [keep.tile([P, PACK, HALF], F32, name=f"taken{h}") for h in range(2)]
+        hid_rows = [keep.tile([P, PACK, HALF], BF16, name=f"hid_rows{h}") for h in range(2)]
+        hid_in = [keep.tile([P, HALF, PACK], BF16, name=f"hid_in{h}", align_bytes=64) for h in range(2)]
+        hid_codes = [keep.tile([P, HALF], U32, name=f"hid_codes{h}", align_bytes=64) for h in range(2)]
+        hid_scales = [keep.tile([P, HALF], U8, name=f"hid_scales{h}", align_bytes=64) for h in range(2)]
+        for h in range(2):
+            for t in range(PACK):
+                nc.scalar.activation(taken[h][:, t, :], sums[h][t], COPY, scale=us_prev[:, t : t + 1])
+            for t in range(PACK):
+                nc.vector.scalar_tensor_tensor(
+                    hid_rows[h][:, t, :], sums[h][t + 1], us_sb[:, t : t + 1], taken[h][:, t, :], ALU.mult, ALU.add
+                )
+        nc.scalar.copy(wb_dealt[:].rearrange("p t m -> p m t"), wb_raw[:].rearrange("p (m t) -> p m t", t=PACK))
+        for h in range(2):
+            interleave(nc.vector.tensor_copy, hid_in[h][:], hid_rows[h][:])
+            nc.vector.quantize_mx(
+                out=hid_codes[h][:].bitcast(E5M2),
+                scales=hid_scales[h][:],
+                in_=hid_in[h][:].rearrange("p j t -> p (j t)"),
+            )
+        for t in (2, 3):
+            nc.scalar.activation(tz_g[:, t, :], tz_rows[1][:, t - 2, :].indirect(list_z[:]), COPY)
+
+        p_sums = [psum.tile([P, PACK, HALF], F32, name=f"p_sums{h}") for h in range(2)]
+        for h in range(2):
+            for t in range(PACK):
+                nc.tensor.matmul_mx(
+                    out=p_sums[h][:, t, :],
+                    lhsT=wb_dealt[:, t, :].bitcast(E4M3),
+                    lhsT_scale=wbs_dealt[:, t, :],
+                    rhs=hid_codes[h][:].bitcast(E5M2),
+                    rhs_scale=hid_scales[h][:],
+                    start=True,
+                    stop=True,
+                )
+
+        floored = [keep.tile([P, PACK, HALF], F32, name=f"floored{h}") for h in range(2)]
+        y = [keep.tile([P, PACK, HALF], F32, name=f"y{h}") for h in range(2)]
+        y_in = [keep.tile([P, HALF, PACK], BF16, name=f"y_in{h}", align_bytes=64) for h in range(2)]
+        y_codes = keep.tile([P, J], U32, name="y_codes", align_bytes=64)
+        y_scales = keep.tile([P, J], U8, name="y_scales", align_bytes=64)
+        for h in range(2):
+            nc.vector.tensor_tensor(floored[h][:], p_sums[h][:], tz_g[:, :, halves[h]], ALU.max)
+        for h in range(2):
+            nc.vector.tensor_tensor(
+                y[h][:], floored[h][:], rw_sb[:, halves[h]].unsqueeze(1).to_broadcast([P, PACK, HALF]), ALU.mult
+            )
+            nc.sync.dma_start(y_v[:, :, halves[h]], y[h][:])
+        interleave(nc.scalar.copy, y_in[0][:], y[0][:])
+        interleave(nc.vector.tensor_copy, y_in[1][:], y[1][:])
+        codes_out = out_1[0].rearrange("p c t -> p (c t)").bitcast(I32)
+        for h in range(2):
+            nc.vector.quantize_mx(
+                out=y_codes[:, halves[h]].bitcast(E4M3),
+                scales=y_scales[:, halves[h]],
+                in_=y_in[h][:].rearrange("p j t -> p (j t)"),
+            )
+            nc.sync.dma_start(codes_out[:, halves[h]], y_codes[:, halves[h]].bitcast(I32))
+        for q in range(4):
+            queue = nc.scalar if q < 2 else nc.sync
+            queue.dma_start(
+                out_2[0, 4 * q : 4 * q + 4, :].bitcast(I32), y_scales[32 * q : 32 * q + 4, :].bitcast(I32)
+            )

@@ -54,16 +54,16 @@ def tile_list_rows_boundedgaps_neighbours_floored_pl_kernel(
         hb_sb = keep.tile([P, PACK], F32, name="hb_sb")
         fk_sb = keep.tile([P, PACK], F32, name="fk_sb")
         us_sb = keep.tile([P, PACK], F32, name="us_sb")
-        us_prev = keep.tile([P, PACK], F32, name="us_prev")
+        us_prev = keep.tile([P, PACK], F32, name="us_prev", tag="after_taken")
         rw_sb = keep.tile([P, J], F32, name="rw_sb")
         w_raw = keep.tile([P, WORD_PAD + R], U32, name="w_raw")
         ws_raw = keep.tile([P, BYTE_PAD + R], U8, name="ws_raw")
+        ws_landed = keep.tile([P, R // 4], I32, name="ws_landed")
         wb_raw = keep.tile([P, N], U32, name="wb_raw")
         wbs_raw = keep.tile([P, N], U8, name="wbs_raw")
         w_dealt = keep.tile([P, PACK + 1, P], U32, name="w_dealt", align_bytes=64)
         ws_dealt = keep.tile([P, PACK + 1, P], U8, name="ws_dealt", align_bytes=64)
         wb_dealt = keep.tile([P, PACK, P], U32, name="wb_dealt", align_bytes=64)
-        wbs_dealt = keep.tile([P, PACK, P], U8, name="wbs_dealt", align_bytes=64)
 
         xa_v = xa.rearrange("(p t) c -> p t c", t=PACK)
         xb_v = xb.rearrange("(p t) c -> p t c", t=PACK)
@@ -71,26 +71,26 @@ def tile_list_rows_boundedgaps_neighbours_floored_pl_kernel(
         y_v = out_0.rearrange("(p t) j -> p t j", t=PACK)
 
         nc.vector.memset(ws_raw[:].bitcast(I32), 0)
-        nc.vector.memset(wbs_raw[:].bitcast(I32), 0)
         nc.vector.memset(w_raw[:, :WORD_PAD], 0)
+        nc.vector.memset(wbs_raw[:].bitcast(I32), 0)
 
         nc.sync.dma_start(list_b[:], offs2)
-        nc.sync.dma_start(xb_rows[0][:], xb_v[:, 0:2, :])
-        nc.gpsimd.dma_start(hb_sb[:], hb.rearrange("(p t) o -> p (t o)", t=PACK))
+        nc.scalar.dma_start(us_sb[:], us.rearrange("o (p t) -> p (o t)", t=PACK))
         nc.gpsimd.dma_start(fk_sb[:], fk.rearrange("(p t) o -> p (t o)", t=PACK))
-        nc.sync.dma_start(xb_rows[1][:], xb_v[:, 2:4, :])
         for q in range(4):
-            nc.scalar.dma_start(
-                ws_raw[32 * q : 32 * q + 4, BYTE_PAD:].bitcast(I32), w_scales[0, 4 * q : 4 * q + 4, :].bitcast(I32)
-            )
+            nc.scalar.dma_start(ws_landed[32 * q : 32 * q + 4, :], w_scales[0, 4 * q : 4 * q + 4, :].bitcast(I32))
+        nc.scalar.activation(us_prev[:], us_sb[:], COPY, scale=NEIGHBOUR)
+        nc.sync.dma_start(xb_rows[0][:], xb_v[:, 0:2, :])
+        nc.sync.dma_start(xb_rows[1][:], xb_v[:, 2:4, :])
+        nc.sync.dma_start(hb_sb[:], hb.rearrange("(p t) o -> p (t o)", t=PACK))
         nc.sync.dma_start(list_a[:], offs)
         nc.sync.dma_start(xa_01[:], xa_v[:, 0:2, :])
         nc.sync.dma_start(xa_2[:], xa_v[:, 2, :])
         nc.sync.dma_start(xa_3[:], xa_v[:, 3, :])
-        nc.gpsimd.dma_start(us_sb[:], us.rearrange("o (p t) -> p (o t)", t=PACK))
         nc.sync.dma_start(
             w_raw[:, WORD_PAD:].bitcast(I32), w_words[0].rearrange("p c t -> p (c t)").bitcast(I32)
         )
+        nc.sync.dma_start(wb_raw[:].bitcast(I32), wb_words[0].rearrange("p c t -> p (c t)").bitcast(I32))
         for q in range(4):
             nc.sync.dma_start(
                 wbs_raw[32 * q : 32 * q + 4, :].bitcast(I32), wb_scales[0, 4 * q : 4 * q + 4, :].bitcast(I32)
@@ -98,45 +98,48 @@ def tile_list_rows_boundedgaps_neighbours_floored_pl_kernel(
         nc.sync.dma_start(list_z[:], offs3)
         for i in range(2):
             nc.sync.dma_start(tz_rows[i][:], tz_v[:, 2 * i : 2 * i + 2, :])
-        nc.sync.dma_start(wb_raw[:].bitcast(I32), wb_words[0].rearrange("p c t -> p (c t)").bitcast(I32))
         nc.sync.dma_start(rw_sb[:], rw[0].partition_broadcast(P))
 
-        xb_g = keep.tile([P, PACK, J], F32, name="xb_g")
-        bound = keep.tile([P, PACK, J], F32, name="bound")
-        xa_g = keep.tile([P, PACK, J], F32, name="xa_g")
-        u_rows = keep.tile([P, PACK, J], BF16, name="u_rows")
-        for t in range(PACK):
-            window = xb_rows[t // 2][:, t % 2, :].indirect(list_b[:])
-            if t % 2 == 0:
-                nc.scalar.activation(xb_g[:, t, :], window, COPY)
-            else:
-                nc.vector.tensor_copy(xb_g[:, t, :], window)
-            nc.vector.tensor_scalar(
-                bound[:, t, :], xb_g[:, t, :], hb_sb[:, t : t + 1], fk_sb[:, t : t + 1], ALU.min, ALU.mult
-            )
-
+        for q in range(4):
+            rows = slice(32 * q, 32 * q + 4)
+            nc.vector.tensor_copy(ws_raw[rows, BYTE_PAD:].bitcast(I32), ws_landed[rows, :])
         nc.vector.tensor_copy(
             ws_dealt[:, 0:PACK, :].rearrange("p t m -> p m t"),
             ws_raw[:, BYTE_PAD - 1 : BYTE_PAD - 1 + R].rearrange("p (m t) -> p m t", t=PACK),
         )
         nc.vector.tensor_copy(ws_dealt[:, PACK, :], ws_raw[:, BYTE_PAD + PACK - 1 :: PACK])
-        nc.vector.tensor_scalar(us_prev[:], us_sb[:], NEIGHBOUR, None, ALU.mult)
+
+        xb_g = keep.tile([P, PACK, J], F32, name="xb_g")
+        bound = keep.tile([P, PACK, J], F32, name="bound")
+        xa_g = keep.tile([P, PACK, J], F32, name="xa_g")
+        u_rows = keep.tile([P, PACK, J], BF16, name="u_rows")
+
+        def gather(on_vector, dst, window, offsets):
+            if on_vector:
+                nc.vector.tensor_copy(dst, window.indirect(offsets))
+            else:
+                nc.scalar.activation(dst, window.indirect(offsets), COPY)
 
         def combine(t, cols):
             nc.vector.scalar_tensor_tensor(
                 u_rows[:, t, cols], xa_g[:, t, cols], fk_sb[:, t : t + 1], bound[:, t, cols], ALU.mult, ALU.subtract
             )
 
-        nc.scalar.activation(xa_g[:, 0, :], xa_01[:, 0, :].indirect(list_a[:]), COPY)
-        nc.vector.tensor_copy(xa_g[:, 1, :], xa_01[:, 1, :].indirect(list_a[:]))
-        combine(0, slice(0, J))
-        combine(1, slice(0, J))
-        nc.scalar.activation(xa_g[:, 2, :], xa_2[:].indirect(list_a[:]), COPY)
-        combine(2, slice(0, J))
+        xa_rows = [xa_01[:, 0, :], xa_01[:, 1, :], xa_2[:], xa_3[:]]
+        for t in range(PACK):
+            gather(t % 2 == 0, xb_g[:, t, :], xb_rows[t // 2][:, t % 2, :], list_b[:])
+        for t in range(PACK):
+            nc.vector.tensor_scalar(
+                bound[:, t, :], xb_g[:, t, :], hb_sb[:, t : t + 1], fk_sb[:, t : t + 1], ALU.min, ALU.mult
+            )
+        for t in range(PACK - 1):
+            gather(t == 1, xa_g[:, t, :], xa_rows[t], list_a[:])
         for h in range(2):
-            nc.scalar.activation(xa_g[:, 3, halves[h]], xa_3[:].indirect(list_a[:, list_halves[h]]), COPY)
+            gather(False, xa_g[:, PACK - 1, halves[h]], xa_rows[PACK - 1], list_a[:, list_halves[h]])
+        for t in range(PACK - 1):
+            combine(t, slice(0, J))
         for h in range(2):
-            combine(3, halves[h])
+            combine(PACK - 1, halves[h])
 
         nc.scalar.copy(
             w_dealt[:, 0:PACK, :].rearrange("p t m -> p m t"),
@@ -144,7 +147,7 @@ def tile_list_rows_boundedgaps_neighbours_floored_pl_kernel(
         )
         nc.scalar.copy(w_dealt[:, PACK, :], w_raw[:, WORD_PAD + PACK - 1 :: PACK])
 
-        u_in = [keep.tile([P, HALF, PACK], BF16, name=f"u_in{h}", align_bytes=64) for h in range(2)]
+        u_in = [keep.tile([P, HALF, PACK], BF16, name=f"u_in{h}", tag=f"u_in{h}", align_bytes=64) for h in range(2)]
         u_codes = [keep.tile([P, HALF], U32, name=f"u_codes{h}", align_bytes=64) for h in range(2)]
         u_scales = [keep.tile([P, HALF], U8, name=f"u_scales{h}", align_bytes=64) for h in range(2)]
         for h in range(2):
@@ -154,10 +157,16 @@ def tile_list_rows_boundedgaps_neighbours_floored_pl_kernel(
                 out=u_codes[h][:].bitcast(E5M2), scales=u_scales[h][:], in_=u_in[h][:].rearrange("p j t -> p (j t)")
             )
 
-        a_before = [psum.tile([P, PACK, HALF], F32, name=f"a_before{h}") for h in range(2)]
-        a_last = [psum.tile([P, HALF], F32, name=f"a_last{h}") for h in range(2)]
-        sums = [[a_before[h][:, s, :] for s in range(PACK)] + [a_last[h][:]] for h in range(2)]
+        nc.scalar.copy(wb_dealt[:].rearrange("p t m -> p m t"), wb_raw[:].rearrange("p (m t) -> p m t", t=PACK))
+        wbs_dealt = keep.tile([P, PACK, P], U8, name="wbs_dealt", tag="u_in1", align_bytes=64)
+        nc.vector.tensor_copy(
+            wbs_dealt[:].rearrange("p t m -> p m t"), wbs_raw[:].rearrange("p (m t) -> p m t", t=PACK)
+        )
+
+        sums = []
         for h in range(2):
+            banks = [psum.tile([P, 2, HALF], F32, name=f"a{h}{b}", tag=f"bank{h}{b}") for b in range(PACK)]
+            sums.append([bank[:, 0, :] for bank in banks] + [banks[-1][:, 1, :]])
             for s in range(PACK + 1):
                 nc.tensor.matmul_mx(
                     out=sums[h][s],
@@ -169,13 +178,6 @@ def tile_list_rows_boundedgaps_neighbours_floored_pl_kernel(
                     stop=True,
                 )
 
-        tz_g = keep.tile([P, PACK, J], F32, name="tz_g")
-        nc.vector.tensor_copy(
-            wbs_dealt[:].rearrange("p t m -> p m t"), wbs_raw[:].rearrange("p (m t) -> p m t", t=PACK)
-        )
-        nc.vector.tensor_copy(tz_g[:, 0, :], tz_rows[0][:, 0, :].indirect(list_z[:]))
-        nc.scalar.activation(tz_g[:, 1, :], tz_rows[0][:, 1, :].indirect(list_z[:]), COPY)
-
         taken = [keep.tile([P, PACK, HALF], F32, name=f"taken{h}") for h in range(2)]
         hid_rows = [keep.tile([P, PACK, HALF], BF16, name=f"hid_rows{h}") for h in range(2)]
         hid_in = [keep.tile([P, HALF, PACK], BF16, name=f"hid_in{h}", align_bytes=64) for h in range(2)]
@@ -184,26 +186,44 @@ def tile_list_rows_boundedgaps_neighbours_floored_pl_kernel(
         for h in range(2):
             for t in range(PACK):
                 nc.scalar.activation(taken[h][:, t, :], sums[h][t], COPY, scale=us_prev[:, t : t + 1])
-            for t in range(PACK):
-                nc.vector.scalar_tensor_tensor(
-                    hid_rows[h][:, t, :], sums[h][t + 1], us_sb[:, t : t + 1], taken[h][:, t, :], ALU.mult, ALU.add
-                )
-        nc.scalar.copy(wb_dealt[:].rearrange("p t m -> p m t"), wb_raw[:].rearrange("p (m t) -> p m t", t=PACK))
-        for h in range(2):
-            interleave(nc.vector.tensor_copy, hid_in[h][:], hid_rows[h][:])
+
+        def hid_row(h, t):
+            nc.vector.scalar_tensor_tensor(
+                hid_rows[h][:, t, :], sums[h][t + 1], us_sb[:, t : t + 1], taken[h][:, t, :], ALU.mult, ALU.add
+            )
+
+        def hid_quantize(h):
             nc.vector.quantize_mx(
                 out=hid_codes[h][:].bitcast(E5M2),
                 scales=hid_scales[h][:],
                 in_=hid_in[h][:].rearrange("p j t -> p (j t)"),
             )
-        for t in (2, 3):
-            nc.scalar.activation(tz_g[:, t, :], tz_rows[1][:, t - 2, :].indirect(list_z[:]), COPY)
 
-        p_sums = [psum.tile([P, PACK, HALF], F32, name=f"p_sums{h}") for h in range(2)]
+        for t in range(PACK):
+            hid_row(0, t)
+        interleave(nc.vector.tensor_copy, hid_in[0][:], hid_rows[0][:])
+        hid_quantize(0)
+        for t in range(PACK):
+            hid_row(1, t)
+        interleave(nc.vector.tensor_copy, hid_in[1][:], hid_rows[1][:])
+        hid_quantize(1)
+
+        tz_g = keep.tile([P, 2, PACK, HALF], F32, name="tz_g", tag="after_taken")
         for h in range(2):
             for t in range(PACK):
+                gather(False, tz_g[:, h, t, :], tz_rows[t // 2][:, t % 2, :], list_z[:, list_halves[h]])
+
+        floored = [keep.tile([P, PACK, HALF], F32, name=f"floored{h}") for h in range(2)]
+        y = [keep.tile([P, PACK, HALF], F32, name=f"y{h}") for h in range(2)]
+        y_in = [keep.tile([P, HALF, PACK], BF16, name=f"y_in{h}", align_bytes=64) for h in range(2)]
+        y_codes = keep.tile([P, J], U32, name="y_codes", align_bytes=64)
+        y_scales = keep.tile([P, J], U8, name="y_scales", align_bytes=64)
+        codes_out = out_1[0].rearrange("p c t -> p (c t)").bitcast(I32)
+
+        def second_product(h, dst):
+            for t in range(PACK):
                 nc.tensor.matmul_mx(
-                    out=p_sums[h][:, t, :],
+                    out=dst[t],
                     lhsT=wb_dealt[:, t, :].bitcast(E4M3),
                     lhsT_scale=wbs_dealt[:, t, :],
                     rhs=hid_codes[h][:].bitcast(E5M2),
@@ -212,28 +232,40 @@ def tile_list_rows_boundedgaps_neighbours_floored_pl_kernel(
                     stop=True,
                 )
 
-        floored = [keep.tile([P, PACK, HALF], F32, name=f"floored{h}") for h in range(2)]
-        y = [keep.tile([P, PACK, HALF], F32, name=f"y{h}") for h in range(2)]
-        y_in = [keep.tile([P, HALF, PACK], BF16, name=f"y_in{h}", align_bytes=64) for h in range(2)]
-        y_codes = keep.tile([P, J], U32, name="y_codes", align_bytes=64)
-        y_scales = keep.tile([P, J], U8, name="y_scales", align_bytes=64)
-        for h in range(2):
-            nc.vector.tensor_tensor(floored[h][:], p_sums[h][:], tz_g[:, :, halves[h]], ALU.max)
-        for h in range(2):
-            nc.vector.tensor_tensor(
-                y[h][:], floored[h][:], rw_sb[:, halves[h]].unsqueeze(1).to_broadcast([P, PACK, HALF]), ALU.mult
-            )
-            nc.sync.dma_start(y_v[:, :, halves[h]], y[h][:])
-        interleave(nc.scalar.copy, y_in[0][:], y[0][:])
-        interleave(nc.vector.tensor_copy, y_in[1][:], y[1][:])
-        codes_out = out_1[0].rearrange("p c t -> p (c t)").bitcast(I32)
-        for h in range(2):
+        def y_quantize(h):
             nc.vector.quantize_mx(
                 out=y_codes[:, halves[h]].bitcast(E4M3),
                 scales=y_scales[:, halves[h]],
                 in_=y_in[h][:].rearrange("p j t -> p (j t)"),
             )
             nc.sync.dma_start(codes_out[:, halves[h]], y_codes[:, halves[h]].bitcast(I32))
+
+        p0 = [psum.tile([P, 2, HALF], F32, name=f"p0{b}", tag=f"bank0{b}") for b in range(2)]
+        second_product(0, [p0[t // 2][:, t % 2, :] for t in range(PACK)])
+        p1 = psum.tile([P, PACK, HALF], F32, name="p1", tag="bank10")
+        second_product(1, [p1[:, t, :] for t in range(PACK)])
+
+        rw_pair = rw_sb[:, halves[0]].unsqueeze(1).to_broadcast([P, 2, HALF])
+        for b in range(2):
+            pair = slice(2 * b, 2 * b + 2)
+            nc.vector.tensor_tensor(floored[0][:, pair, :], p0[b][:], tz_g[:, 0, pair, :], ALU.max)
+        for b in range(2):
+            pair = slice(2 * b, 2 * b + 2)
+            nc.vector.tensor_tensor(y[0][:, pair, :], floored[0][:, pair, :], rw_pair, ALU.mult)
+        nc.sync.dma_start(y_v[:, :, halves[0]], y[0][:])
+        interleave(nc.scalar.copy, y_in[0][:], y[0][:])
+
+        quarters = [slice(0, HALF // 2), slice(HALF // 2, HALF)]
+        for cols in quarters:
+            nc.vector.tensor_tensor(floored[1][:, :, cols], p1[:, :, cols], tz_g[:, 1, :, cols], ALU.max)
+        for cols in quarters:
+            weight = rw_sb[:, halves[1]][:, cols].unsqueeze(1).to_broadcast([P, PACK, HALF // 2])
+            nc.vector.tensor_tensor(y[1][:, :, cols], floored[1][:, :, cols], weight, ALU.mult)
+        nc.sync.dma_start(y_v[:, :, halves[1]], y[1][:])
+        y_quantize(0)
+        interleave(nc.scalar.copy, y_in[1][:, quarters[0], :], y[1][:, :, quarters[0]])
+        interleave(nc.vector.tensor_copy, y_in[1][:, quarters[1], :], y[1][:, :, quarters[1]])
+        y_quantize(1)
         for q in range(4):
             queue = nc.scalar if q < 2 else nc.sync
             queue.dma_start(

from contextlib import ExitStack

import concourse.mybir as mybir

K, T, J, R, N = 512, 512, 256, 512, 512
FLOPS = 2 * J * K * R + 2 * N * R * J

F32 = mybir.dt.float32
BF16 = mybir.dt.bfloat16
I32 = mybir.dt.int32
U32 = mybir.dt.uint32
U16 = mybir.dt.uint16
U8 = mybir.dt.uint8
E4M3 = mybir.dt.float8_e4m3fn_x4
E5M2 = mybir.dt.float8_e5m2_x4
ALU = mybir.AluOpType
COPY = mybir.ActivationFunctionType.Copy

P = 128
PACK = 4
HALF = J // 2
LIST_COLS = J // 16
WORD_PAD = 8
BYTE_PAD = 32
NEIGHBOUR = -0.7


def interleave(engine_copy, dst, src):
    engine_copy(
        out=dst.rearrange("p (c i) t -> p c t i", i=4),
        in_=src.rearrange("p t (c i) -> p c t i", i=4),
    )


def tile_list_rows_boundedgaps_neighbours_floored_pl_kernel(
    tc, xa, xb, hb, fk, w_words, w_scales, us, wb_words, wb_scales, tz, rw, offs, offs2, offs3, out_0, out_1, out_2
):
    nc = tc.nc
    halves = [slice(h * HALF, (h + 1) * HALF) for h in range(2)]
    list_halves = [slice(h * LIST_COLS // 2, (h + 1) * LIST_COLS // 2) for h in range(2)]

    with ExitStack() as ctx:
        keep = ctx.enter_context(tc.tile_pool(name="keep", bufs=1))
        psum = ctx.enter_context(tc.psum_pool(name="psum", bufs=1))

        list_a = keep.tile([P, LIST_COLS], U16, name="list_a")
        list_b = keep.tile([P, LIST_COLS], U16, name="list_b")
        list_z = keep.tile([P, LIST_COLS], U16, name="list_z")
        xb_rows = [keep.tile([P, 2, T], F32, name=f"xb_rows{i}") for i in range(2)]
        xa_01 = keep.tile([P, 2, T], F32, name="xa_01")
        xa_2 = keep.tile([P, T], F32, name="xa_2")
        xa_3 = keep.tile([P, T], F32, name="xa_3")
        tz_rows = [keep.tile([P, 2, T], F32, name=f"tz_rows{i}") for i in range(2)]
        hb_sb = keep.tile([P, PACK], F32, name="hb_sb")
        fk_sb = keep.tile([P, PACK], F32, name="fk_sb")
        us_sb = keep.tile([P, PACK], F32, name="us_sb")
        us_prev = keep.tile([P, PACK], F32, name="us_prev", tag="after_taken")
        rw_sb = keep.tile([P, J], F32, name="rw_sb")
        w_raw = keep.tile([P, WORD_PAD + R], U32, name="w_raw")
        ws_raw = keep.tile([P, BYTE_PAD + R], U8, name="ws_raw")
        ws_landed = keep.tile([P, R // 4], I32, name="ws_landed")
        wb_raw = keep.tile([P, N], U32, name="wb_raw")
        wbs_raw = keep.tile([P, N], U8, name="wbs_raw")
        w_dealt = keep.tile([P, PACK + 1, P], U32, name="w_dealt", align_bytes=64)
        ws_dealt = keep.tile([P, PACK + 1, P], U8, name="ws_dealt", align_bytes=64)
        wb_dealt = keep.tile([P, PACK, P], U32, name="wb_dealt", align_bytes=64)

        xa_v = xa.rearrange("(p t) c -> p t c", t=PACK)
        xb_v = xb.rearrange("(p t) c -> p t c", t=PACK)
        tz_v = tz.rearrange("(p t) c -> p t c", t=PACK)
        y_v = out_0.rearrange("(p t) j -> p t j", t=PACK)

        nc.vector.memset(ws_raw[:].bitcast(I32), 0)
        nc.vector.memset(w_raw[:, :WORD_PAD], 0)
        nc.vector.memset(wbs_raw[:].bitcast(I32), 0)

        nc.sync.dma_start(list_b[:], offs2)
        nc.scalar.dma_start(us_sb[:], us.rearrange("o (p t) -> p (o t)", t=PACK))
        nc.gpsimd.dma_start(fk_sb[:], fk.rearrange("(p t) o -> p (t o)", t=PACK))
        for q in range(4):
            nc.scalar.dma_start(ws_landed[32 * q : 32 * q + 4, :], w_scales[0, 4 * q : 4 * q + 4, :].bitcast(I32))
        nc.scalar.activation(us_prev[:], us_sb[:], COPY, scale=NEIGHBOUR)
        nc.sync.dma_start(xb_rows[0][:], xb_v[:, 0:2, :])
        nc.sync.dma_start(xb_rows[1][:], xb_v[:, 2:4, :])
        nc.sync.dma_start(hb_sb[:], hb.rearrange("(p t) o -> p (t o)", t=PACK))
        nc.sync.dma_start(list_a[:], offs)
        nc.sync.dma_start(xa_01[:], xa_v[:, 0:2, :])
        nc.sync.dma_start(xa_2[:], xa_v[:, 2, :])
        nc.sync.dma_start(xa_3[:], xa_v[:, 3, :])
        nc.sync.dma_start(
            w_raw[:, WORD_PAD:].bitcast(I32), w_words[0].rearrange("p c t -> p (c t)").bitcast(I32)
        )
        nc.sync.dma_start(wb_raw[:].bitcast(I32), wb_words[0].rearrange("p c t -> p (c t)").bitcast(I32))
        for q in range(4):
            nc.sync.dma_start(
                wbs_raw[32 * q : 32 * q + 4, :].bitcast(I32), wb_scales[0, 4 * q : 4 * q + 4, :].bitcast(I32)
            )
        nc.sync.dma_start(list_z[:], offs3)
        for i in range(2):
            nc.sync.dma_start(tz_rows[i][:], tz_v[:, 2 * i : 2 * i + 2, :])
        nc.sync.dma_start(rw_sb[:], rw[0].partition_broadcast(P))

        for q in range(4):
            rows = slice(32 * q, 32 * q + 4)
            nc.vector.tensor_copy(ws_raw[rows, BYTE_PAD:].bitcast(I32), ws_landed[rows, :])
        nc.vector.tensor_copy(
            ws_dealt[:, 0:PACK, :].rearrange("p t m -> p m t"),
            ws_raw[:, BYTE_PAD - 1 : BYTE_PAD - 1 + R].rearrange("p (m t) -> p m t", t=PACK),
        )
        nc.vector.tensor_copy(ws_dealt[:, PACK, :], ws_raw[:, BYTE_PAD + PACK - 1 :: PACK])

        xb_g = keep.tile([P, PACK, J], F32, name="xb_g")
        bound = keep.tile([P, PACK, J], F32, name="bound")
        xa_g = keep.tile([P, PACK, J], F32, name="xa_g")
        u_rows = keep.tile([P, PACK, J], BF16, name="u_rows")

        def gather(on_vector, dst, window, offsets):
            if on_vector:
                nc.vector.tensor_copy(dst, window.indirect(offsets))
            else:
                nc.scalar.activation(dst, window.indirect(offsets), COPY)

        def combine(t, cols):
            nc.vector.scalar_tensor_tensor(
                u_rows[:, t, cols], xa_g[:, t, cols], fk_sb[:, t : t + 1], bound[:, t, cols], ALU.mult, ALU.subtract
            )

        xa_rows = [xa_01[:, 0, :], xa_01[:, 1, :], xa_2[:], xa_3[:]]
        for t in range(PACK):
            gather(t % 2 == 0, xb_g[:, t, :], xb_rows[t // 2][:, t % 2, :], list_b[:])
        for t in range(PACK):
            nc.vector.tensor_scalar(
                bound[:, t, :], xb_g[:, t, :], hb_sb[:, t : t + 1], fk_sb[:, t : t + 1], ALU.min, ALU.mult
            )
        for t in range(PACK - 1):
            gather(t == 1, xa_g[:, t, :], xa_rows[t], list_a[:])
        for h in range(2):
            gather(False, xa_g[:, PACK - 1, halves[h]], xa_rows[PACK - 1], list_a[:, list_halves[h]])
        for t in range(PACK - 1):
            combine(t, slice(0, J))
        for h in range(2):
            combine(PACK - 1, halves[h])

        nc.scalar.copy(
            w_dealt[:, 0:PACK, :].rearrange("p t m -> p m t"),
            w_raw[:, WORD_PAD - 1 : WORD_PAD - 1 + R].rearrange("p (m t) -> p m t", t=PACK),
        )
        nc.scalar.copy(w_dealt[:, PACK, :], w_raw[:, WORD_PAD + PACK - 1 :: PACK])

        u_in = [keep.tile([P, HALF, PACK], BF16, name=f"u_in{h}", tag=f"u_in{h}", align_bytes=64) for h in range(2)]
        u_codes = [keep.tile([P, HALF], U32, name=f"u_codes{h}", align_bytes=64) for h in range(2)]
        u_scales = [keep.tile([P, HALF], U8, name=f"u_scales{h}", align_bytes=64) for h in range(2)]
        for h in range(2):
            interleave(nc.vector.tensor_copy, u_in[h][:], u_rows[:, :, halves[h]])
        for h in range(2):
            nc.vector.quantize_mx(
                out=u_codes[h][:].bitcast(E5M2), scales=u_scales[h][:], in_=u_in[h][:].rearrange("p j t -> p (j t)")
            )

        nc.scalar.copy(wb_dealt[:].rearrange("p t m -> p m t"), wb_raw[:].rearrange("p (m t) -> p m t", t=PACK))
        wbs_dealt = keep.tile([P, PACK, P], U8, name="wbs_dealt", tag="u_in1", align_bytes=64)
        nc.vector.tensor_copy(
            wbs_dealt[:].rearrange("p t m -> p m t"), wbs_raw[:].rearrange("p (m t) -> p m t", t=PACK)
        )

        sums = []
        for h in range(2):
            banks = [psum.tile([P, 2, HALF], F32, name=f"a{h}{b}", tag=f"bank{h}{b}") for b in range(PACK)]
            sums.append([bank[:, 0, :] for bank in banks] + [banks[-1][:, 1, :]])
            for s in range(PACK + 1):
                nc.tensor.matmul_mx(
                    out=sums[h][s],
                    lhsT=w_dealt[:, s, :].bitcast(E5M2),
                    lhsT_scale=ws_dealt[:, s, :],
                    rhs=u_codes[h][:].bitcast(E5M2),
                    rhs_scale=u_scales[h][:],
                    start=True,
                    stop=True,
                )

        taken = [keep.tile([P, PACK, HALF], F32, name=f"taken{h}") for h in range(2)]
        hid_rows = [keep.tile([P, PACK, HALF], BF16, name=f"hid_rows{h}") for h in range(2)]
        hid_in = [keep.tile([P, HALF, PACK], BF16, name=f"hid_in{h}", align_bytes=64) for h in range(2)]
        hid_codes = [keep.tile([P, HALF], U32, name=f"hid_codes{h}", align_bytes=64) for h in range(2)]
        hid_scales = [keep.tile([P, HALF], U8, name=f"hid_scales{h}", align_bytes=64) for h in range(2)]
        for h in range(2):
            for t in range(PACK):
                nc.scalar.activation(taken[h][:, t, :], sums[h][t], COPY, scale=us_prev[:, t : t + 1])

        def hid_row(h, t):
            nc.vector.scalar_tensor_tensor(
                hid_rows[h][:, t, :], sums[h][t + 1], us_sb[:, t : t + 1], taken[h][:, t, :], ALU.mult, ALU.add
            )

        def hid_quantize(h):
            nc.vector.quantize_mx(
                out=hid_codes[h][:].bitcast(E5M2),
                scales=hid_scales[h][:],
                in_=hid_in[h][:].rearrange("p j t -> p (j t)"),
            )

        for t in range(PACK):
            hid_row(0, t)
        interleave(nc.vector.tensor_copy, hid_in[0][:], hid_rows[0][:])
        hid_quantize(0)
        for t in range(PACK):
            hid_row(1, t)
        interleave(nc.vector.tensor_copy, hid_in[1][:], hid_rows[1][:])
        hid_quantize(1)

        tz_g = keep.tile([P, 2, PACK, HALF], F32, name="tz_g", tag="after_taken")
        for h in range(2):
            for t in range(PACK):
                gather(False, tz_g[:, h, t, :], tz_rows[t // 2][:, t % 2, :], list_z[:, list_halves[h]])

        floored = [keep.tile([P, PACK, HALF], F32, name=f"floored{h}") for h in range(2)]
        y = [keep.tile([P, PACK, HALF], F32, name=f"y{h}") for h in range(2)]
        y_in = [keep.tile([P, HALF, PACK], BF16, name=f"y_in{h}", align_bytes=64) for h in range(2)]
        y_codes = keep.tile([P, J], U32, name="y_codes", align_bytes=64)
        y_scales = keep.tile([P, J], U8, name="y_scales", align_bytes=64)
        codes_out = out_1[0].rearrange("p c t -> p (c t)").bitcast(I32)

        def second_product(h, dst):
            for t in range(PACK):
                nc.tensor.matmul_mx(
                    out=dst[t],
                    lhsT=wb_dealt[:, t, :].bitcast(E4M3),
                    lhsT_scale=wbs_dealt[:, t, :],
                    rhs=hid_codes[h][:].bitcast(E5M2),
                    rhs_scale=hid_scales[h][:],
                    start=True,
                    stop=True,
                )

        def y_quantize(h):
            nc.vector.quantize_mx(
                out=y_codes[:, halves[h]].bitcast(E4M3),
                scales=y_scales[:, halves[h]],
                in_=y_in[h][:].rearrange("p j t -> p (j t)"),
            )
            nc.sync.dma_start(codes_out[:, halves[h]], y_codes[:, halves[h]].bitcast(I32))

        p0 = [psum.tile([P, 2, HALF], F32, name=f"p0{b}", tag=f"bank0{b}") for b in range(2)]
        second_product(0, [p0[t // 2][:, t % 2, :] for t in range(PACK)])
        p1 = psum.tile([P, PACK, HALF], F32, name="p1", tag="bank10")
        second_product(1, [p1[:, t, :] for t in range(PACK)])

        rw_pair = rw_sb[:, halves[0]].unsqueeze(1).to_broadcast([P, 2, HALF])
        for b in range(2):
            pair = slice(2 * b, 2 * b + 2)
            nc.vector.tensor_tensor(floored[0][:, pair, :], p0[b][:], tz_g[:, 0, pair, :], ALU.max)
        for b in range(2):
            pair = slice(2 * b, 2 * b + 2)
            nc.vector.tensor_tensor(y[0][:, pair, :], floored[0][:, pair, :], rw_pair, ALU.mult)
        nc.sync.dma_start(y_v[:, :, halves[0]], y[0][:])
        interleave(nc.scalar.copy, y_in[0][:], y[0][:])

        quarters = [slice(0, HALF // 2), slice(HALF // 2, HALF)]
        for cols in quarters:
            nc.vector.tensor_tensor(floored[1][:, :, cols], p1[:, :, cols], tz_g[:, 1, :, cols], ALU.max)
        for cols in quarters:
            weight = rw_sb[:, halves[1]][:, cols].unsqueeze(1).to_broadcast([P, PACK, HALF // 2])
            nc.vector.tensor_tensor(y[1][:, :, cols], floored[1][:, :, cols], weight, ALU.mult)
        nc.sync.dma_start(y_v[:, :, halves[1]], y[1][:])
        y_quantize(0)
        interleave(nc.scalar.copy, y_in[1][:, quarters[0], :], y[1][:, :, quarters[0]])
        interleave(nc.vector.tensor_copy, y_in[1][:, quarters[1], :], y[1][:, :, quarters[1]])
        y_quantize(1)
        for q in range(4):
            queue = nc.scalar if q < 2 else nc.sync
            queue.dma_start(
                out_2[0, 4 * q : 4 * q + 4, :].bitcast(I32), y_scales[32 * q : 32 * q + 4, :].bitcast(I32)
            )
